import numpy as np
import ml_dtypes


def mxq(x, axis, fmt="e4m3"):
    dtype, down = {"e4m3": (ml_dtypes.float8_e4m3fn, 7), "e5m2": (ml_dtypes.float8_e5m2, 14)}[fmt]
    v = np.moveaxis(np.asarray(x, np.float32).astype(ml_dtypes.bfloat16).astype(np.float64), axis, -1)
    blocks = v.reshape(v.shape[:-1] + (-1, 32))
    amax = np.abs(blocks).max(-1, keepdims=True)
    byte = np.maximum(np.where(amax > 0, np.frexp(amax)[1] - 1 + 127, 0) - down, 1)
    scale = np.exp2(byte - 127.0)
    codes = (blocks / scale).astype(np.float32).astype(dtype).astype(np.float64)
    return np.moveaxis((codes * scale).reshape(v.shape), -1, axis)


WIDE = False


def mx_kscale(k):
    if not WIDE:
        return np.ones(k)
    levels = np.array([10, -10, 5, -5, 0])
    if k % 512:
        return np.exp2(np.random.permutation(np.resize(levels, k // 32))).repeat(32)
    a = np.empty((k // 512, 16))
    for p in range(k // 512):
        a[p, :8] = np.random.permutation(np.resize(levels, 8))
        for g in range(8):
            far = levels[np.abs(levels - a[p, g]) >= 10]
            a[p, g + 8] = far[np.random.randint(len(far))]
    return np.exp2(a.ravel()).repeat(32)


def f64(x):
    return np.asarray(x).astype(np.float64)


def striped(idx):
    return np.tile(idx.reshape(-1, 16).T, (8, 1)).astype(np.uint16)


def unstriped(offs):
    return offs[:16].T.reshape(-1).astype(np.int64)


def striped8(idx):
    return np.concatenate([x.reshape(-1, 16).T for x in idx]).astype(np.uint16)


def runs(offs, k):
    lists = np.stack([offs[16 * r : 16 * r + 16].T.reshape(-1) for r in range(8)]).astype(np.int64)
    return lists[np.arange(k) % 512 // 64]


def pack_weight(w):
    k, n = w.shape
    w = f64(np.asarray(w, np.float32).astype(ml_dtypes.bfloat16)).reshape(k // 32, 32, n)
    amax = np.abs(w).max(1)
    byte = np.clip(np.where(amax > 0, np.frexp(amax)[1] - 1 + 127 - 7, 1), 1, 254)
    scaled = (w * np.exp2(127.0 - byte)[:, None, :]).reshape(k, n).astype(np.float32)
    words = np.ascontiguousarray(scaled.reshape(k // 512, 128, 4, n).transpose(0, 1, 3, 2)).astype(ml_dtypes.float8_e4m3fn).view(np.uint8)
    return words, np.ascontiguousarray(byte.astype(np.uint8).reshape(k // 512, 16, n))


def unpack_weight(words, scales):
    g, p, n, _ = words.shape
    vals = np.ascontiguousarray(words).view(ml_dtypes.float8_e4m3fn).astype(np.float64) * np.repeat(np.exp2(scales.astype(np.float64) - 127.0), 8, axis=1)[..., None]
    return vals.transpose(0, 1, 3, 2).reshape(g * 512, n)


K, T, S, H, W, C = 512, 2048, 512, 512, 256, 512


def setup_inputs():
    n = np.random.standard_normal
    s = mx_kscale(K)[:, None]
    packed_xT = pack_weight(n((K, T)) * s)
    perm = np.random.permutation(S)
    return {
        "x_words": packed_xT[0],
        "x_scales": packed_xT[1],
        "w1": (n((K, H)) / np.sqrt(K) / s).astype(np.float32),
        "gs": (np.random.uniform(0.5, 1.5, (K, 1)) / s).astype(np.float32),
        "offs": striped(np.random.permutation(T)[:S]),
        "n1": striped(perm[:W]),
        "n2": striped(perm[W:]),
        "ca": striped(np.random.permutation(T)[:C]),
        "hc": striped8(np.random.randint(0, T, (8, C))),
        "n3": striped(np.random.permutation(S)),
        "n4": striped(np.random.permutation(S)),
        "n5": striped(np.random.permutation(S)),
        "n6": striped(np.random.permutation(S)),
    }


def reference(x_words, x_scales, w1, gs, offs, n1, n2, ca, hc, n3, n4, n5, n6):
    x_ca = unpack_weight(x_words, x_scales)[:, unstriped(ca)]
    xq = unpack_weight(x_words, x_scales)[:, unstriped(offs)]
    y = mxq(f64(w1), 0, "e4m3").T @ xq
    pa = y[:, unstriped(n1)]
    pb = y[:, unstriped(n2)]
    rb = np.minimum(pa, pb)
    ra = np.maximum(pa, pb)
    ds = np.zeros((H, S))
    ds[:, unstriped(n1)] = ra
    dt = ds.copy()
    dt[:, unstriped(n2)] = rb
    z = f64(gs) * dt
    zq = mxq(z, 0, "e4m3")
    a = 0.0625 * (x_ca.T @ zq)
    x_hc = unpack_weight(x_words, x_scales)[np.arange(K)[:, None], runs(hc, K)]
    b = 0.0625 * (x_hc.T @ zq)
    return np.maximum(a[:, unstriped(n3)] + b[:, unstriped(n5)], a[:, unstriped(n4)] + b[:, unstriped(n6)])

@@ -1,0 +1,157 @@
+from contextlib import ExitStack
+
+import concourse.mybir as mybir
+
+F32 = mybir.dt.float32
+BF16 = mybir.dt.bfloat16
+I32 = mybir.dt.int32
+U32 = mybir.dt.uint32
+U16 = mybir.dt.uint16
+U8 = mybir.dt.uint8
+FP8X4 = mybir.dt.float8_e4m3fn_x4
+ALU = mybir.AluOpType
+COPY = mybir.ActivationFunctionType.Copy
+
+P = 128
+PACK = 4
+K, T, S, W = 512, 2048, 512, 256
+SPARE = 8
+FLOPS = 3 * 2 * K * S * S
+
+
+def tile_picked_cdhpathborder_none_p_kernel(
+    tc, x_words, x_scales, w1, gs, offs, n1, n2, ca, hc, n3, n4, n5, n6, out
+):
+    nc = tc.nc
+    with ExitStack() as ctx:
+        keep = ctx.enter_context(tc.tile_pool(name="keep", bufs=1))
+        psum = ctx.enter_context(tc.psum_pool(name="psum", bufs=4))
+
+        def load_list(name, src):
+            tile = keep.tile(list(src.shape), U16, name=name)
+            nc.sync.dma_start(tile[:], src)
+            return tile
+
+        byte_table = keep.tile([P, T], U8, name="byte_table")
+        nc.vector.memset(byte_table[:].bitcast(I32), 0)
+        l_offs = load_list("l_offs", offs)
+        l_ca = load_list("l_ca", ca)
+        l_hc = load_list("l_hc", hc)
+        rows = x_scales[0].bitcast(I32)
+        for u in range(4):
+            step = 2 if u < 2 else 4
+            nc.sync.dma_start(byte_table[u : P : 8 * step, :].bitcast(I32), rows[u:16:step, :])
+        w_raw = keep.tile([P, PACK, K], F32, name="w_raw")
+        nc.sync.dma_start(w_raw[:], w1.rearrange("(p j) c -> p j c", j=PACK))
+        word_table = keep.tile([P, T], U32, name="word_table")
+        nc.sync.dma_start(word_table[:].bitcast(I32), x_words[0].rearrange("p n t -> p (n t)").bitcast(I32))
+        l_n1 = load_list("l_n1", n1)
+        l_n2 = load_list("l_n2", n2)
+        gain = keep.tile([P, PACK], F32, name="gain")
+        nc.sync.dma_start(gain[:], gs.rearrange("(p t) one -> p (t one)", t=PACK))
+        l_n3 = load_list("l_n3", n3)
+        l_n4 = load_list("l_n4", n4)
+        l_n5 = load_list("l_n5", n5)
+        l_n6 = load_list("l_n6", n6)
+
+        def pick(name, table, lst, dtype):
+            tile = keep.tile([P, S], dtype, name=name, align_bytes=64)
+            nc.vector.tensor_copy(tile[:], table[:].indirect(lst[:]))
+            return tile
+
+        xq_bytes = pick("xq_bytes", byte_table, l_offs, U8)
+        hc_raw = pick("hc_raw", byte_table, l_hc, U8)
+        ca_bytes = pick("ca_bytes", byte_table, l_ca, U8)
+
+        hc_bytes = keep.tile([P, S], U8, name="hc_bytes", align_bytes=64)
+        nc.gpsimd.memset(hc_bytes[:], 0)
+        for u in range(4):
+            src = u if u < 2 else 14 + u
+            nc.sync.dma_start(hc_bytes[u:P:32, :].bitcast(I32), hc_raw[src:P:32, :].bitcast(I32))
+
+        w_bf = keep.tile([P, PACK * K], BF16, name="w_bf", align_bytes=64)
+        nc.scalar.copy(
+            w_bf[:].rearrange("p (t m j) -> p m j t", t=PACK, j=PACK),
+            w_raw[:].rearrange("p j (m t) -> p m j t", t=PACK),
+        )
+        w_codes = keep.tile([P, K], U32, name="w_codes", align_bytes=64)
+        w_scales = keep.tile([P, K], U8, name="w_scales", align_bytes=64)
+        nc.vector.quantize_mx(out=w_codes[:].bitcast(FP8X4), scales=w_scales[:], in_=w_bf[:])
+
+        xq_words = pick("xq_words", word_table, l_offs, U32)
+        ca_words = pick("ca_words", word_table, l_ca, U32)
+        hc_words = pick("hc_words", word_table, l_hc, U32)
+
+        def product(name, l_words, l_bytes, block, r_words, r_bytes):
+            cols = slice(block * P, (block + 1) * P)
+            acc = psum.tile([P, S], F32, name=name)
+            nc.tensor.matmul_mx(
+                out=acc[:],
+                lhsT=l_words[:, cols].bitcast(FP8X4),
+                lhsT_scale=l_bytes[:, cols],
+                rhs=r_words[:].bitcast(FP8X4),
+                rhs_scale=r_bytes[:],
+                start=True,
+                stop=True,
+            )
+            return acc
+
+        z_bf = keep.tile([P, S, PACK], BF16, name="z_bf", align_bytes=64)
+        pairs, sorts, dts = {}, {}, {}
+
+        def fetch(t):
+            acc = product("y_acc", w_codes, w_scales, t, xq_words, xq_bytes)
+            y = keep.tile([P, S], F32, name="y%d" % t)
+            nc.scalar.copy(y[:], acc[:])
+            pairs[t] = keep.tile([P, 2, W], F32, name="pair%d" % t)
+            nc.scalar.activation(pairs[t][:, 0, :], y[:].indirect(l_n1[:]), COPY)
+            nc.scalar.activation(pairs[t][:, 1, :], y[:].indirect(l_n2[:]), COPY)
+
+        def order_and_put_larger(t):
+            sorts[t] = keep.tile([P, 2, W], F32, name="sort%d" % t)
+            nc.vector.tensor_tensor(sorts[t][:, 0, :], pairs[t][:, 0, :], pairs[t][:, 1, :], ALU.max)
+            nc.vector.tensor_tensor(sorts[t][:, 1, :], pairs[t][:, 0, :], pairs[t][:, 1, :], ALU.min)
+            dts[t] = keep.tile([P, S], F32, name="dt%d" % t)
+            nc.vector.tensor_copy(dts[t][:].indirect(l_n1[:]), sorts[t][:, 0, :])
+
+        def put_smaller(t):
+            nc.scalar.activation(dts[t][:].indirect(l_n2[:]), sorts[t][:, 1, :], COPY)
+
+        def weigh(t):
+            nc.vector.tensor_scalar(z_bf[:, :, t], dts[t][:], gain[:, t : t + 1], None, ALU.mult)
+
+        for t in range(PACK):
+            fetch(t)
+            order_and_put_larger(t)
+            if t >= 2:
+                put_smaller(t - 2)
+        put_smaller(2)
+        put_smaller(3)
+        for t in range(PACK):
+            weigh(t)
+
+        z_codes = keep.tile([P, S], U32, name="z_codes", align_bytes=64)
+        z_scales = keep.tile([P, S], U8, name="z_scales", align_bytes=64)
+        nc.vector.quantize_mx(
+            out=z_codes[:].bitcast(FP8X4), scales=z_scales[:], in_=z_bf[:].rearrange("p s t -> p (s t)")
+        )
+
+        for r in range(S // P):
+            a_acc = product("ab_acc", ca_words, ca_bytes, r, z_codes, z_scales)
+            b_acc = product("ab_acc", hc_words, hc_bytes, r, z_codes, z_scales)
+            a = keep.tile([P, S + SPARE], F32, name="a%d" % r)
+            b = keep.tile([P, S + SPARE], F32, name="b%d" % r)
+            nc.scalar.activation(a[:, :S], a_acc[:], COPY, scale=0.0625)
+            if r < 2:
+                nc.vector.tensor_scalar(b[:, :S], b_acc[:], 0.0625, None, ALU.mult)
+            else:
+                nc.scalar.activation(b[:, :S], b_acc[:], COPY, scale=0.0625)
+            ga = keep.tile([P, 2, S], F32, name="ga%d" % r)
+            nc.scalar.activation(ga[:, 0, :], a[:].indirect(l_n3[:]), COPY)
+            nc.scalar.activation(ga[:, 1, :], a[:].indirect(l_n4[:]), COPY)
+            sums = keep.tile([P, 2, S], F32, name="sums%d" % r)
+            nc.vector.tensor_tensor(sums[:, 0, :], b[:].indirect(l_n5[:]), ga[:, 0, :], ALU.add)
+            nc.vector.tensor_tensor(sums[:, 1, :], b[:].indirect(l_n6[:]), ga[:, 1, :], ALU.add)
+            res = keep.tile([P, S], F32, name="res%d" % r)
+            nc.vector.tensor_tensor(res[:], sums[:, 0, :], sums[:, 1, :], ALU.max)
+            nc.sync.dma_start(out[r * P : (r + 1) * P, :], res[:])

@@ -16,6 +16,9 @@ P = 128
 PACK = 4
 K, T, S, W = 512, 2048, 512, 256
 SPARE = 8
+W_SPLIT = 88
+HALF = S // 2
+LAST = 128
 FLOPS = 3 * 2 * K * S * S
 
 
@@ -41,7 +44,7 @@ def tile_picked_cdhpathborder_none_p_kernel(
         for u in range(4):
             step = 2 if u < 2 else 4
             nc.sync.dma_start(byte_table[u : P : 8 * step, :].bitcast(I32), rows[u:16:step, :])
-        w_raw = keep.tile([P, PACK, K], F32, name="w_raw")
+        w_raw = keep.tile([P, PACK, K], F32, name="w_raw", tag="slot_a", align_bytes=64)
         nc.sync.dma_start(w_raw[:], w1.rearrange("(p j) c -> p j c", j=PACK))
         word_table = keep.tile([P, T], U32, name="word_table")
         nc.sync.dma_start(word_table[:].bitcast(I32), x_words[0].rearrange("p n t -> p (n t)").bitcast(I32))
@@ -54,8 +57,8 @@ def tile_picked_cdhpathborder_none_p_kernel(
         l_n5 = load_list("l_n5", n5)
         l_n6 = load_list("l_n6", n6)
 
-        def pick(name, table, lst, dtype):
-            tile = keep.tile([P, S], dtype, name=name, align_bytes=64)
+        def pick(name, table, lst, dtype, tag=None):
+            tile = keep.tile([P, S], dtype, name=name, tag=tag or name, align_bytes=64)
             nc.vector.tensor_copy(tile[:], table[:].indirect(lst[:]))
             return tile
 
@@ -69,43 +72,52 @@ def tile_picked_cdhpathborder_none_p_kernel(
             src = u if u < 2 else 14 + u
             nc.sync.dma_start(hc_bytes[u:P:32, :].bitcast(I32), hc_raw[src:P:32, :].bitcast(I32))
 
-        w_bf = keep.tile([P, PACK * K], BF16, name="w_bf", align_bytes=64)
-        nc.scalar.copy(
-            w_bf[:].rearrange("p (t m j) -> p m j t", t=PACK, j=PACK),
-            w_raw[:].rearrange("p j (m t) -> p m j t", t=PACK),
-        )
+        w_bf = keep.tile([P, PACK * K], BF16, name="w_bf", tag="slot_b", align_bytes=64)
+        w_dst = w_bf[:].rearrange("p (t m j) -> p m j t", t=PACK, j=PACK)
+        w_src = w_raw[:].rearrange("p j (m t) -> p m j t", t=PACK)
+        nc.scalar.copy(w_dst[:, :W_SPLIT], w_src[:, :W_SPLIT])
+        nc.vector.tensor_copy(w_dst[:, W_SPLIT:], w_src[:, W_SPLIT:])
         w_codes = keep.tile([P, K], U32, name="w_codes", align_bytes=64)
         w_scales = keep.tile([P, K], U8, name="w_scales", align_bytes=64)
         nc.vector.quantize_mx(out=w_codes[:].bitcast(FP8X4), scales=w_scales[:], in_=w_bf[:])
 
-        xq_words = pick("xq_words", word_table, l_offs, U32)
-        ca_words = pick("ca_words", word_table, l_ca, U32)
-        hc_words = pick("hc_words", word_table, l_hc, U32)
+        xq_words = keep.tile([P, S], U32, name="xq_words", align_bytes=64)
+        for lo in (0, HALF):
+            nc.vector.tensor_copy(
+                xq_words[:, lo : lo + HALF], word_table[:].indirect(l_offs[:, lo // 16 : (lo + HALF) // 16])
+            )
+        ca_words = pick("ca_words", word_table, l_ca, U32, "slot_a")
+        hc_words = pick("hc_words", word_table, l_hc, U32, "slot_b")
 
-        def product(name, l_words, l_bytes, block, r_words, r_bytes):
-            cols = slice(block * P, (block + 1) * P)
-            acc = psum.tile([P, S], F32, name=name)
+        def product(acc, l_words, l_bytes, block, r_words, r_bytes, cols):
+            rows_of = slice(block * P, (block + 1) * P)
             nc.tensor.matmul_mx(
-                out=acc[:],
-                lhsT=l_words[:, cols].bitcast(FP8X4),
-                lhsT_scale=l_bytes[:, cols],
-                rhs=r_words[:].bitcast(FP8X4),
-                rhs_scale=r_bytes[:],
+                out=acc[:, cols],
+                lhsT=l_words[:, rows_of].bitcast(FP8X4),
+                lhsT_scale=l_bytes[:, rows_of],
+                rhs=r_words[:, cols].bitcast(FP8X4),
+                rhs_scale=r_bytes[:, cols],
                 start=True,
                 stop=True,
             )
-            return acc
 
-        z_bf = keep.tile([P, S, PACK], BF16, name="z_bf", align_bytes=64)
+        whole = slice(0, S)
+        halves = [slice(0, HALF), slice(HALF, S)]
+        z_pairs = keep.tile([P, 2, 2 * S], BF16, name="z_pairs", align_bytes=64)
         pairs, sorts, dts = {}, {}, {}
 
         def fetch(t):
-            acc = product("y_acc", w_codes, w_scales, t, xq_words, xq_bytes)
+            acc = psum.tile([P, S], F32, name="y_acc", tag="first")
+            for cols in halves if t == 0 else [whole]:
+                product(acc, w_codes, w_scales, t, xq_words, xq_bytes, cols)
             y = keep.tile([P, S], F32, name="y%d" % t)
             nc.scalar.copy(y[:], acc[:])
             pairs[t] = keep.tile([P, 2, W], F32, name="pair%d" % t)
             nc.scalar.activation(pairs[t][:, 0, :], y[:].indirect(l_n1[:]), COPY)
-            nc.scalar.activation(pairs[t][:, 1, :], y[:].indirect(l_n2[:]), COPY)
+            if t == 0:
+                nc.vector.tensor_copy(pairs[t][:, 1, :], y[:].indirect(l_n2[:]))
+            else:
+                nc.scalar.activation(pairs[t][:, 1, :], y[:].indirect(l_n2[:]), COPY)
 
         def order_and_put_larger(t):
             sorts[t] = keep.tile([P, 2, W], F32, name="sort%d" % t)
@@ -114,44 +126,65 @@ def tile_picked_cdhpathborder_none_p_kernel(
             dts[t] = keep.tile([P, S], F32, name="dt%d" % t)
             nc.vector.tensor_copy(dts[t][:].indirect(l_n1[:]), sorts[t][:, 0, :])
 
-        def put_smaller(t):
-            nc.scalar.activation(dts[t][:].indirect(l_n2[:]), sorts[t][:, 1, :], COPY)
+        def put_smaller(t, lo, hi):
+            nc.scalar.activation(dts[t][:].indirect(l_n2[:, lo // 16 : hi // 16]), sorts[t][:, 1, lo:hi], COPY)
 
         def weigh(t):
-            nc.vector.tensor_scalar(z_bf[:, :, t], dts[t][:], gain[:, t : t + 1], None, ALU.mult)
+            dst = z_pairs[:, t // 2, :].rearrange("p (s e) -> p s e", e=2)[:, :, t % 2]
+            nc.vector.tensor_scalar(dst, dts[t][:], gain[:, t : t + 1], None, ALU.mult)
 
         for t in range(PACK):
             fetch(t)
             order_and_put_larger(t)
             if t >= 2:
-                put_smaller(t - 2)
-        put_smaller(2)
-        put_smaller(3)
-        for t in range(PACK):
-            weigh(t)
+                put_smaller(t - 2, 0, W)
+        put_smaller(2, 0, W // 2)
+        put_smaller(3, 0, W)
+        weigh(0)
+        weigh(1)
+        nc.vector.tensor_copy(dts[2][:].indirect(l_n2[:, W // 32 :]), sorts[2][:, 1, W // 2 :])
+        weigh(2)
+        weigh(3)
 
+        z_words = z_pairs[:].bitcast(F32).rearrange("p u s -> p s u")
         z_codes = keep.tile([P, S], U32, name="z_codes", align_bytes=64)
         z_scales = keep.tile([P, S], U8, name="z_scales", align_bytes=64)
-        nc.vector.quantize_mx(
-            out=z_codes[:].bitcast(FP8X4), scales=z_scales[:], in_=z_bf[:].rearrange("p s t -> p (s t)")
-        )
+        z_bf = [keep.tile([P, HALF * PACK], BF16, name="z_bf%d" % h, align_bytes=64) for h in range(2)]
+        woven = [z[:].bitcast(F32).rearrange("p (s u) -> p s u", u=2) for z in z_bf]
+        nc.vector.tensor_copy(woven[0], z_words[:, halves[0], :])
+        nc.scalar.copy(woven[1], z_words[:, halves[1], :])
+        for h in range(2):
+            nc.vector.quantize_mx(
+                out=z_codes[:, halves[h]].bitcast(FP8X4), scales=z_scales[:, halves[h]], in_=z_bf[h][:]
+            )
 
-        for r in range(S // P):
-            a_acc = product("ab_acc", ca_words, ca_bytes, r, z_codes, z_scales)
-            b_acc = product("ab_acc", hc_words, hc_bytes, r, z_codes, z_scales)
+        blocks = S // P
+        a_acc = [psum.tile([P, S], F32, name="a_acc%d" % r, tag="second") for r in range(blocks)]
+        b_acc = [psum.tile([P, S], F32, name="b_acc%d" % r, tag="first") for r in range(blocks)]
+        for cols in halves:
+            product(a_acc[0], ca_words, ca_bytes, 0, z_codes, z_scales, cols)
+        for r in range(blocks):
+            product(b_acc[r], hc_words, hc_bytes, r, z_codes, z_scales, whole)
+            if r >= 1:
+                product(a_acc[r], ca_words, ca_bytes, r, z_codes, z_scales, whole)
+
+        for r in range(blocks):
             a = keep.tile([P, S + SPARE], F32, name="a%d" % r)
             b = keep.tile([P, S + SPARE], F32, name="b%d" % r)
-            nc.scalar.activation(a[:, :S], a_acc[:], COPY, scale=0.0625)
-            if r < 2:
-                nc.vector.tensor_scalar(b[:, :S], b_acc[:], 0.0625, None, ALU.mult)
+            nc.scalar.activation(a[:, :S], a_acc[r][:], COPY, scale=0.0625)
+            if r < 3:
+                nc.vector.tensor_scalar(b[:, :S], b_acc[r][:], 0.0625, None, ALU.mult)
             else:
-                nc.scalar.activation(b[:, :S], b_acc[:], COPY, scale=0.0625)
+                nc.scalar.activation(b[:, :S], b_acc[r][:], COPY, scale=0.0625)
             ga = keep.tile([P, 2, S], F32, name="ga%d" % r)
-            nc.scalar.activation(ga[:, 0, :], a[:].indirect(l_n3[:]), COPY)
-            nc.scalar.activation(ga[:, 1, :], a[:].indirect(l_n4[:]), COPY)
             sums = keep.tile([P, 2, S], F32, name="sums%d" % r)
-            nc.vector.tensor_tensor(sums[:, 0, :], b[:].indirect(l_n5[:]), ga[:, 0, :], ALU.add)
-            nc.vector.tensor_tensor(sums[:, 1, :], b[:].indirect(l_n6[:]), ga[:, 1, :], ALU.add)
             res = keep.tile([P, S], F32, name="res%d" % r)
-            nc.vector.tensor_tensor(res[:], sums[:, 0, :], sums[:, 1, :], ALU.max)
-            nc.sync.dma_start(out[r * P : (r + 1) * P, :], res[:])
+            pieces = {0: halves, blocks - 1: [slice(0, S - LAST), slice(S - LAST, S)]}.get(r, [whole])
+            for cols in pieces:
+                entries = slice(cols.start // 16, cols.stop // 16)
+                nc.scalar.activation(ga[:, 0, cols], a[:].indirect(l_n3[:, entries]), COPY)
+                nc.scalar.activation(ga[:, 1, cols], a[:].indirect(l_n4[:, entries]), COPY)
+                nc.vector.tensor_tensor(sums[:, 0, cols], b[:].indirect(l_n5[:, entries]), ga[:, 0, cols], ALU.add)
+                nc.vector.tensor_tensor(sums[:, 1, cols], b[:].indirect(l_n6[:, entries]), ga[:, 1, cols], ALU.add)
+                nc.vector.tensor_tensor(res[:, cols], sums[:, 0, cols], sums[:, 1, cols], ALU.max)
+                nc.sync.dma_start(out[r * P : (r + 1) * P, cols], res[:, cols])

@@ -16,9 +16,8 @@ P = 128
 PACK = 4
 K, T, S, W = 512, 2048, 512, 256
 SPARE = 8
-W_SPLIT = 88
 HALF = S // 2
-LAST = 128
+SHARE = 64
 FLOPS = 3 * 2 * K * S * S
 
 
@@ -72,22 +71,26 @@ def tile_picked_cdhpathborder_none_p_kernel(
             src = u if u < 2 else 14 + u
             nc.sync.dma_start(hc_bytes[u:P:32, :].bitcast(I32), hc_raw[src:P:32, :].bitcast(I32))
 
-        w_bf = keep.tile([P, PACK * K], BF16, name="w_bf", tag="slot_b", align_bytes=64)
-        w_dst = w_bf[:].rearrange("p (t m j) -> p m j t", t=PACK, j=PACK)
         w_src = w_raw[:].rearrange("p j (m t) -> p m j t", t=PACK)
-        nc.scalar.copy(w_dst[:, :W_SPLIT], w_src[:, :W_SPLIT])
-        nc.vector.tensor_copy(w_dst[:, W_SPLIT:], w_src[:, W_SPLIT:])
         w_codes = keep.tile([P, K], U32, name="w_codes", align_bytes=64)
         w_scales = keep.tile([P, K], U8, name="w_scales", align_bytes=64)
-        nc.vector.quantize_mx(out=w_codes[:].bitcast(FP8X4), scales=w_scales[:], in_=w_bf[:])
+        w_low = keep.tile([P, 2 * K], BF16, name="w_low", align_bytes=64)
+        w_high = keep.tile([P, 2 * K], BF16, name="w_high", tag="slot_b", align_bytes=64)
+        nc.scalar.copy(w_low[:].rearrange("p (t m j) -> p m j t", t=2, j=PACK), w_src[:, :, :, 0:2])
+        nc.scalar.copy(w_high[:].rearrange("p (t m j) -> p m j t", t=2, j=PACK), w_src[:, :, :, 2:4])
+        nc.vector.quantize_mx(out=w_codes[:, :HALF].bitcast(FP8X4), scales=w_scales[:, :HALF], in_=w_low[:])
 
-        xq_words = keep.tile([P, S], U32, name="xq_words", align_bytes=64)
+        xq_words = keep.tile([P, S], U32, name="xq_words", tag="slot_a", align_bytes=64)
         for lo in (0, HALF):
             nc.vector.tensor_copy(
                 xq_words[:, lo : lo + HALF], word_table[:].indirect(l_offs[:, lo // 16 : (lo + HALF) // 16])
             )
-        ca_words = pick("ca_words", word_table, l_ca, U32, "slot_a")
-        hc_words = pick("hc_words", word_table, l_hc, U32, "slot_b")
+        nc.vector.quantize_mx(out=w_codes[:, HALF:].bitcast(FP8X4), scales=w_scales[:, HALF:], in_=w_high[:])
+        cand_words = keep.tile([P, 2 * S], U32, name="cand_words", tag="slot_b", align_bytes=64)
+        ca_words = cand_words[:, :S]
+        hc_words = cand_words[:, S:]
+        nc.vector.tensor_copy(ca_words, word_table[:].indirect(l_ca[:]))
+        nc.vector.tensor_copy(hc_words, word_table[:].indirect(l_hc[:]))
 
         def product(acc, l_words, l_bytes, block, r_words, r_bytes, cols):
             rows_of = slice(block * P, (block + 1) * P)
@@ -103,7 +106,6 @@ def tile_picked_cdhpathborder_none_p_kernel(
 
         whole = slice(0, S)
         halves = [slice(0, HALF), slice(HALF, S)]
-        z_pairs = keep.tile([P, 2, 2 * S], BF16, name="z_pairs", align_bytes=64)
         pairs, sorts, dts = {}, {}, {}
 
         def fetch(t):
@@ -112,12 +114,9 @@ def tile_picked_cdhpathborder_none_p_kernel(
                 product(acc, w_codes, w_scales, t, xq_words, xq_bytes, cols)
             y = keep.tile([P, S], F32, name="y%d" % t)
             nc.scalar.copy(y[:], acc[:])
-            pairs[t] = keep.tile([P, 2, W], F32, name="pair%d" % t)
+            pairs[t] = keep.tile([P, 2, W], F32, name="pair%d" % t, tag="pair%d" % t, align_bytes=64)
             nc.scalar.activation(pairs[t][:, 0, :], y[:].indirect(l_n1[:]), COPY)
-            if t == 0:
-                nc.vector.tensor_copy(pairs[t][:, 1, :], y[:].indirect(l_n2[:]))
-            else:
-                nc.scalar.activation(pairs[t][:, 1, :], y[:].indirect(l_n2[:]), COPY)
+            nc.scalar.activation(pairs[t][:, 1, :], y[:].indirect(l_n2[:]), COPY)
 
         def order_and_put_larger(t):
             sorts[t] = keep.tile([P, 2, W], F32, name="sort%d" % t)
@@ -136,13 +135,14 @@ def tile_picked_cdhpathborder_none_p_kernel(
         for t in range(PACK):
             fetch(t)
             order_and_put_larger(t)
-            if t >= 2:
-                put_smaller(t - 2, 0, W)
-        put_smaller(2, 0, W // 2)
+        put_smaller(0, 0, W)
+        put_smaller(1, 0, W)
+        put_smaller(2, 0, W - SHARE)
         put_smaller(3, 0, W)
+        z_pairs = keep.tile([P, 2, 2 * S], BF16, name="z_pairs", tag="pair3", align_bytes=64)
         weigh(0)
         weigh(1)
-        nc.vector.tensor_copy(dts[2][:].indirect(l_n2[:, W // 32 :]), sorts[2][:, 1, W // 2 :])
+        nc.vector.tensor_copy(dts[2][:].indirect(l_n2[:, (W - SHARE) // 16 :]), sorts[2][:, 1, W - SHARE :])
         weigh(2)
         weigh(3)
 
@@ -159,32 +159,36 @@ def tile_picked_cdhpathborder_none_p_kernel(
             )
 
         blocks = S // P
-        a_acc = [psum.tile([P, S], F32, name="a_acc%d" % r, tag="second") for r in range(blocks)]
-        b_acc = [psum.tile([P, S], F32, name="b_acc%d" % r, tag="first") for r in range(blocks)]
-        for cols in halves:
-            product(a_acc[0], ca_words, ca_bytes, 0, z_codes, z_scales, cols)
+        accs = {}
         for r in range(blocks):
-            product(b_acc[r], hc_words, hc_bytes, r, z_codes, z_scales, whole)
-            if r >= 1:
-                product(a_acc[r], ca_words, ca_bytes, r, z_codes, z_scales, whole)
+            for cols in halves if r == 0 else [whole]:
+                for side, words, planes in (("a", ca_words, ca_bytes), ("b", hc_words, hc_bytes)):
+                    acc = psum.tile([P, S], F32, name="acc", tag="first" if r in (1, 2) else "second")
+                    product(acc, words, planes, r, z_codes, z_scales, cols)
+                    accs[side, r, cols.start] = acc
 
         for r in range(blocks):
             a = keep.tile([P, S + SPARE], F32, name="a%d" % r)
             b = keep.tile([P, S + SPARE], F32, name="b%d" % r)
-            nc.scalar.activation(a[:, :S], a_acc[r][:], COPY, scale=0.0625)
-            if r < 3:
-                nc.vector.tensor_scalar(b[:, :S], b_acc[r][:], 0.0625, None, ALU.mult)
-            else:
-                nc.scalar.activation(b[:, :S], b_acc[r][:], COPY, scale=0.0625)
+            for cols in halves if r == 0 else [whole]:
+                nc.scalar.activation(a[:, cols], accs["a", r, cols.start][:, cols], COPY, scale=0.0625)
+                if r < 3:
+                    nc.vector.tensor_scalar(b[:, cols], accs["b", r, cols.start][:, cols], 0.0625, None, ALU.mult)
+                else:
+                    nc.scalar.activation(b[:, cols], accs["b", r, cols.start][:, cols], COPY, scale=0.0625)
             ga = keep.tile([P, 2, S], F32, name="ga%d" % r)
             sums = keep.tile([P, 2, S], F32, name="sums%d" % r)
             res = keep.tile([P, S], F32, name="res%d" % r)
-            pieces = {0: halves, blocks - 1: [slice(0, S - LAST), slice(S - LAST, S)]}.get(r, [whole])
-            for cols in pieces:
+            for cols in halves if r in (0, blocks - 1) else [whole]:
                 entries = slice(cols.start // 16, cols.stop // 16)
                 nc.scalar.activation(ga[:, 0, cols], a[:].indirect(l_n3[:, entries]), COPY)
                 nc.scalar.activation(ga[:, 1, cols], a[:].indirect(l_n4[:, entries]), COPY)
                 nc.vector.tensor_tensor(sums[:, 0, cols], b[:].indirect(l_n5[:, entries]), ga[:, 0, cols], ALU.add)
-                nc.vector.tensor_tensor(sums[:, 1, cols], b[:].indirect(l_n6[:, entries]), ga[:, 1, cols], ALU.add)
+                if r == blocks - 1 and cols.stop == S:
+                    gb = keep.tile([P, HALF], F32, name="gb")
+                    nc.scalar.activation(gb[:], b[:].indirect(l_n6[:, entries]), COPY)
+                    nc.vector.tensor_tensor(sums[:, 1, cols], gb[:], ga[:, 1, cols], ALU.add)
+                else:
+                    nc.vector.tensor_tensor(sums[:, 1, cols], b[:].indirect(l_n6[:, entries]), ga[:, 1, cols], ALU.add)
                 nc.vector.tensor_tensor(res[:, cols], sums[:, 0, cols], sums[:, 1, cols], ALU.max)
                 nc.sync.dma_start(out[r * P : (r + 1) * P, cols], res[:, cols])

@@ -17,7 +17,7 @@ PACK = 4
 K, T, S, W = 512, 2048, 512, 256
 SPARE = 8
 HALF = S // 2
-SHARE = 64
+SHARE = 128
 FLOPS = 3 * 2 * K * S * S
 
 
@@ -43,10 +43,10 @@ def tile_picked_cdhpathborder_none_p_kernel(
         for u in range(4):
             step = 2 if u < 2 else 4
             nc.sync.dma_start(byte_table[u : P : 8 * step, :].bitcast(I32), rows[u:16:step, :])
-        w_raw = keep.tile([P, PACK, K], F32, name="w_raw", tag="slot_a", align_bytes=64)
-        nc.sync.dma_start(w_raw[:], w1.rearrange("(p j) c -> p j c", j=PACK))
         word_table = keep.tile([P, T], U32, name="word_table")
         nc.sync.dma_start(word_table[:].bitcast(I32), x_words[0].rearrange("p n t -> p (n t)").bitcast(I32))
+        w_raw = keep.tile([P, PACK, K], F32, name="w_raw")
+        nc.sync.dma_start(w_raw[:], w1.rearrange("(p j) c -> p j c", j=PACK))
         l_n1 = load_list("l_n1", n1)
         l_n2 = load_list("l_n2", n2)
         gain = keep.tile([P, PACK], F32, name="gain")
@@ -66,37 +66,35 @@ def tile_picked_cdhpathborder_none_p_kernel(
         ca_bytes = pick("ca_bytes", byte_table, l_ca, U8)
 
         hc_bytes = keep.tile([P, S], U8, name="hc_bytes", align_bytes=64)
-        nc.gpsimd.memset(hc_bytes[:], 0)
+        nc.vector.memset(hc_bytes[:].bitcast(I32), 0)
         for u in range(4):
             src = u if u < 2 else 14 + u
             nc.sync.dma_start(hc_bytes[u:P:32, :].bitcast(I32), hc_raw[src:P:32, :].bitcast(I32))
 
+        xq_words = pick("xq_words", word_table, l_offs, U32)
+        ca_early = keep.tile([P, HALF], U32, name="ca_early", align_bytes=64)
+        nc.vector.tensor_copy(ca_early[:], word_table[:].indirect(l_ca[:, : HALF // 16]))
         w_src = w_raw[:].rearrange("p j (m t) -> p m j t", t=PACK)
         w_codes = keep.tile([P, K], U32, name="w_codes", align_bytes=64)
         w_scales = keep.tile([P, K], U8, name="w_scales", align_bytes=64)
-        w_low = keep.tile([P, 2 * K], BF16, name="w_low", align_bytes=64)
-        w_high = keep.tile([P, 2 * K], BF16, name="w_high", tag="slot_b", align_bytes=64)
+        w_low = keep.tile([P, 2 * K], BF16, name="w_low", tag="slot_b", align_bytes=64)
+        w_high = keep.tile([P, 2 * K], BF16, name="w_high", align_bytes=64)
         nc.scalar.copy(w_low[:].rearrange("p (t m j) -> p m j t", t=2, j=PACK), w_src[:, :, :, 0:2])
         nc.scalar.copy(w_high[:].rearrange("p (t m j) -> p m j t", t=2, j=PACK), w_src[:, :, :, 2:4])
         nc.vector.quantize_mx(out=w_codes[:, :HALF].bitcast(FP8X4), scales=w_scales[:, :HALF], in_=w_low[:])
-
-        xq_words = keep.tile([P, S], U32, name="xq_words", tag="slot_a", align_bytes=64)
-        for lo in (0, HALF):
-            nc.vector.tensor_copy(
-                xq_words[:, lo : lo + HALF], word_table[:].indirect(l_offs[:, lo // 16 : (lo + HALF) // 16])
-            )
+        late = keep.tile([P, HALF + S], U32, name="late", tag="slot_b", align_bytes=64)
+        nc.vector.tensor_copy(late[:, :HALF], word_table[:].indirect(l_ca[:, HALF // 16 :]))
+        nc.vector.tensor_copy(late[:, HALF:], word_table[:].indirect(l_hc[:]))
+        ca_words = [ca_early[:, :P], ca_early[:, P:], late[:, :P], late[:, P:HALF]]
+        hc_words = [late[:, HALF + r * P : HALF + (r + 1) * P] for r in range(S // P)]
+        w_words = [w_codes[:, t * P : (t + 1) * P] for t in range(PACK)]
         nc.vector.quantize_mx(out=w_codes[:, HALF:].bitcast(FP8X4), scales=w_scales[:, HALF:], in_=w_high[:])
-        cand_words = keep.tile([P, 2 * S], U32, name="cand_words", tag="slot_b", align_bytes=64)
-        ca_words = cand_words[:, :S]
-        hc_words = cand_words[:, S:]
-        nc.vector.tensor_copy(ca_words, word_table[:].indirect(l_ca[:]))
-        nc.vector.tensor_copy(hc_words, word_table[:].indirect(l_hc[:]))
 
         def product(acc, l_words, l_bytes, block, r_words, r_bytes, cols):
             rows_of = slice(block * P, (block + 1) * P)
             nc.tensor.matmul_mx(
                 out=acc[:, cols],
-                lhsT=l_words[:, rows_of].bitcast(FP8X4),
+                lhsT=l_words[block].bitcast(FP8X4),
                 lhsT_scale=l_bytes[:, rows_of],
                 rhs=r_words[:, cols].bitcast(FP8X4),
                 rhs_scale=r_bytes[:, cols],
@@ -109,14 +107,17 @@ def tile_picked_cdhpathborder_none_p_kernel(
         pairs, sorts, dts = {}, {}, {}
 
         def fetch(t):
-            acc = psum.tile([P, S], F32, name="y_acc", tag="first")
-            for cols in halves if t == 0 else [whole]:
-                product(acc, w_codes, w_scales, t, xq_words, xq_bytes, cols)
             y = keep.tile([P, S], F32, name="y%d" % t)
-            nc.scalar.copy(y[:], acc[:])
+            for cols in halves if t == 0 else [whole]:
+                acc = psum.tile([P, S], F32, name="y_acc", tag="first")
+                product(acc, w_words, w_scales, t, xq_words, xq_bytes, cols)
+                nc.scalar.copy(y[:, cols], acc[:, cols])
             pairs[t] = keep.tile([P, 2, W], F32, name="pair%d" % t, tag="pair%d" % t, align_bytes=64)
             nc.scalar.activation(pairs[t][:, 0, :], y[:].indirect(l_n1[:]), COPY)
-            nc.scalar.activation(pairs[t][:, 1, :], y[:].indirect(l_n2[:]), COPY)
+            if t == 0:
+                nc.vector.tensor_copy(pairs[t][:, 1, :], y[:].indirect(l_n2[:]))
+            else:
+                nc.scalar.activation(pairs[t][:, 1, :], y[:].indirect(l_n2[:]), COPY)
 
         def order_and_put_larger(t):
             sorts[t] = keep.tile([P, 2, W], F32, name="sort%d" % t)

from contextlib import ExitStack

import concourse.mybir as mybir

F32 = mybir.dt.float32
BF16 = mybir.dt.bfloat16
I32 = mybir.dt.int32
U32 = mybir.dt.uint32
U16 = mybir.dt.uint16
U8 = mybir.dt.uint8
FP8X4 = mybir.dt.float8_e4m3fn_x4
ALU = mybir.AluOpType
COPY = mybir.ActivationFunctionType.Copy

P = 128
PACK = 4
K, T, S, W = 512, 2048, 512, 256
SPARE = 8
HALF = S // 2
SHARE = 128
FLOPS = 3 * 2 * K * S * S


def tile_picked_cdhpathborder_none_p_kernel(
    tc, x_words, x_scales, w1, gs, offs, n1, n2, ca, hc, n3, n4, n5, n6, out
):
    nc = tc.nc
    with ExitStack() as ctx:
        keep = ctx.enter_context(tc.tile_pool(name="keep", bufs=1))
        psum = ctx.enter_context(tc.psum_pool(name="psum", bufs=4))

        def load_list(name, src):
            tile = keep.tile(list(src.shape), U16, name=name)
            nc.sync.dma_start(tile[:], src)
            return tile

        byte_table = keep.tile([P, T], U8, name="byte_table")
        nc.vector.memset(byte_table[:].bitcast(I32), 0)
        l_offs = load_list("l_offs", offs)
        l_ca = load_list("l_ca", ca)
        l_hc = load_list("l_hc", hc)
        rows = x_scales[0].bitcast(I32)
        for u in range(4):
            step = 2 if u < 2 else 4
            nc.sync.dma_start(byte_table[u : P : 8 * step, :].bitcast(I32), rows[u:16:step, :])
        word_table = keep.tile([P, T], U32, name="word_table")
        nc.sync.dma_start(word_table[:].bitcast(I32), x_words[0].rearrange("p n t -> p (n t)").bitcast(I32))
        w_raw = keep.tile([P, PACK, K], F32, name="w_raw")
        nc.sync.dma_start(w_raw[:], w1.rearrange("(p j) c -> p j c", j=PACK))
        l_n1 = load_list("l_n1", n1)
        l_n2 = load_list("l_n2", n2)
        gain = keep.tile([P, PACK], F32, name="gain")
        nc.sync.dma_start(gain[:], gs.rearrange("(p t) one -> p (t one)", t=PACK))
        l_n3 = load_list("l_n3", n3)
        l_n4 = load_list("l_n4", n4)
        l_n5 = load_list("l_n5", n5)
        l_n6 = load_list("l_n6", n6)

        def pick(name, table, lst, dtype, tag=None):
            tile = keep.tile([P, S], dtype, name=name, tag=tag or name, align_bytes=64)
            nc.vector.tensor_copy(tile[:], table[:].indirect(lst[:]))
            return tile

        xq_bytes = pick("xq_bytes", byte_table, l_offs, U8)
        hc_raw = pick("hc_raw", byte_table, l_hc, U8)
        ca_bytes = pick("ca_bytes", byte_table, l_ca, U8)

        hc_bytes = keep.tile([P, S], U8, name="hc_bytes", align_bytes=64)
        nc.vector.memset(hc_bytes[:].bitcast(I32), 0)
        for u in range(4):
            src = u if u < 2 else 14 + u
            nc.sync.dma_start(hc_bytes[u:P:32, :].bitcast(I32), hc_raw[src:P:32, :].bitcast(I32))

        xq_words = pick("xq_words", word_table, l_offs, U32)
        ca_early = keep.tile([P, HALF], U32, name="ca_early", align_bytes=64)
        nc.vector.tensor_copy(ca_early[:], word_table[:].indirect(l_ca[:, : HALF // 16]))
        w_src = w_raw[:].rearrange("p j (m t) -> p m j t", t=PACK)
        w_codes = keep.tile([P, K], U32, name="w_codes", align_bytes=64)
        w_scales = keep.tile([P, K], U8, name="w_scales", align_bytes=64)
        w_low = keep.tile([P, 2 * K], BF16, name="w_low", tag="slot_b", align_bytes=64)
        w_high = keep.tile([P, 2 * K], BF16, name="w_high", align_bytes=64)
        nc.scalar.copy(w_low[:].rearrange("p (t m j) -> p m j t", t=2, j=PACK), w_src[:, :, :, 0:2])
        nc.scalar.copy(w_high[:].rearrange("p (t m j) -> p m j t", t=2, j=PACK), w_src[:, :, :, 2:4])
        nc.vector.quantize_mx(out=w_codes[:, :HALF].bitcast(FP8X4), scales=w_scales[:, :HALF], in_=w_low[:])
        late = keep.tile([P, HALF + S], U32, name="late", tag="slot_b", align_bytes=64)
        nc.vector.tensor_copy(late[:, :HALF], word_table[:].indirect(l_ca[:, HALF // 16 :]))
        nc.vector.tensor_copy(late[:, HALF:], word_table[:].indirect(l_hc[:]))
        ca_words = [ca_early[:, :P], ca_early[:, P:], late[:, :P], late[:, P:HALF]]
        hc_words = [late[:, HALF + r * P : HALF + (r + 1) * P] for r in range(S // P)]
        w_words = [w_codes[:, t * P : (t + 1) * P] for t in range(PACK)]
        nc.vector.quantize_mx(out=w_codes[:, HALF:].bitcast(FP8X4), scales=w_scales[:, HALF:], in_=w_high[:])

        def product(acc, l_words, l_bytes, block, r_words, r_bytes, cols):
            rows_of = slice(block * P, (block + 1) * P)
            nc.tensor.matmul_mx(
                out=acc[:, cols],
                lhsT=l_words[block].bitcast(FP8X4),
                lhsT_scale=l_bytes[:, rows_of],
                rhs=r_words[:, cols].bitcast(FP8X4),
                rhs_scale=r_bytes[:, cols],
                start=True,
                stop=True,
            )

        whole = slice(0, S)
        halves = [slice(0, HALF), slice(HALF, S)]
        pairs, sorts, dts = {}, {}, {}

        def fetch(t):
            y = keep.tile([P, S], F32, name="y%d" % t)
            for cols in halves if t == 0 else [whole]:
                acc = psum.tile([P, S], F32, name="y_acc", tag="first")
                product(acc, w_words, w_scales, t, xq_words, xq_bytes, cols)
                nc.scalar.copy(y[:, cols], acc[:, cols])
            pairs[t] = keep.tile([P, 2, W], F32, name="pair%d" % t, tag="pair%d" % t, align_bytes=64)
            nc.scalar.activation(pairs[t][:, 0, :], y[:].indirect(l_n1[:]), COPY)
            if t == 0:
                nc.vector.tensor_copy(pairs[t][:, 1, :], y[:].indirect(l_n2[:]))
            else:
                nc.scalar.activation(pairs[t][:, 1, :], y[:].indirect(l_n2[:]), COPY)

        def order_and_put_larger(t):
            sorts[t] = keep.tile([P, 2, W], F32, name="sort%d" % t)
            nc.vector.tensor_tensor(sorts[t][:, 0, :], pairs[t][:, 0, :], pairs[t][:, 1, :], ALU.max)
            nc.vector.tensor_tensor(sorts[t][:, 1, :], pairs[t][:, 0, :], pairs[t][:, 1, :], ALU.min)
            dts[t] = keep.tile([P, S], F32, name="dt%d" % t)
            nc.vector.tensor_copy(dts[t][:].indirect(l_n1[:]), sorts[t][:, 0, :])

        def put_smaller(t, lo, hi):
            nc.scalar.activation(dts[t][:].indirect(l_n2[:, lo // 16 : hi // 16]), sorts[t][:, 1, lo:hi], COPY)

        def weigh(t):
            dst = z_pairs[:, t // 2, :].rearrange("p (s e) -> p s e", e=2)[:, :, t % 2]
            nc.vector.tensor_scalar(dst, dts[t][:], gain[:, t : t + 1], None, ALU.mult)

        for t in range(PACK):
            fetch(t)
            order_and_put_larger(t)
        put_smaller(0, 0, W)
        put_smaller(1, 0, W)
        put_smaller(2, 0, W - SHARE)
        put_smaller(3, 0, W)
        z_pairs = keep.tile([P, 2, 2 * S], BF16, name="z_pairs", tag="pair3", align_bytes=64)
        weigh(0)
        weigh(1)
        nc.vector.tensor_copy(dts[2][:].indirect(l_n2[:, (W - SHARE) // 16 :]), sorts[2][:, 1, W - SHARE :])
        weigh(2)
        weigh(3)

        z_words = z_pairs[:].bitcast(F32).rearrange("p u s -> p s u")
        z_codes = keep.tile([P, S], U32, name="z_codes", align_bytes=64)
        z_scales = keep.tile([P, S], U8, name="z_scales", align_bytes=64)
        z_bf = [keep.tile([P, HALF * PACK], BF16, name="z_bf%d" % h, align_bytes=64) for h in range(2)]
        woven = [z[:].bitcast(F32).rearrange("p (s u) -> p s u", u=2) for z in z_bf]
        nc.vector.tensor_copy(woven[0], z_words[:, halves[0], :])
        nc.scalar.copy(woven[1], z_words[:, halves[1], :])
        for h in range(2):
            nc.vector.quantize_mx(
                out=z_codes[:, halves[h]].bitcast(FP8X4), scales=z_scales[:, halves[h]], in_=z_bf[h][:]
            )

        blocks = S // P
        accs = {}
        for r in range(blocks):
            for cols in halves if r == 0 else [whole]:
                for side, words, planes in (("a", ca_words, ca_bytes), ("b", hc_words, hc_bytes)):
                    acc = psum.tile([P, S], F32, name="acc", tag="first" if r in (1, 2) else "second")
                    product(acc, words, planes, r, z_codes, z_scales, cols)
                    accs[side, r, cols.start] = acc

        for r in range(blocks):
            a = keep.tile([P, S + SPARE], F32, name="a%d" % r)
            b = keep.tile([P, S + SPARE], F32, name="b%d" % r)
            for cols in halves if r == 0 else [whole]:
                nc.scalar.activation(a[:, cols], accs["a", r, cols.start][:, cols], COPY, scale=0.0625)
                if r < 3:
                    nc.vector.tensor_scalar(b[:, cols], accs["b", r, cols.start][:, cols], 0.0625, None, ALU.mult)
                else:
                    nc.scalar.activation(b[:, cols], accs["b", r, cols.start][:, cols], COPY, scale=0.0625)
            ga = keep.tile([P, 2, S], F32, name="ga%d" % r)
            sums = keep.tile([P, 2, S], F32, name="sums%d" % r)
            res = keep.tile([P, S], F32, name="res%d" % r)
            for cols in halves if r in (0, blocks - 1) else [whole]:
                entries = slice(cols.start // 16, cols.stop // 16)
                nc.scalar.activation(ga[:, 0, cols], a[:].indirect(l_n3[:, entries]), COPY)
                nc.scalar.activation(ga[:, 1, cols], a[:].indirect(l_n4[:, entries]), COPY)
                nc.vector.tensor_tensor(sums[:, 0, cols], b[:].indirect(l_n5[:, entries]), ga[:, 0, cols], ALU.add)
                if r == blocks - 1 and cols.stop == S:
                    gb = keep.tile([P, HALF], F32, name="gb")
                    nc.scalar.activation(gb[:], b[:].indirect(l_n6[:, entries]), COPY)
                    nc.vector.tensor_tensor(sums[:, 1, cols], gb[:], ga[:, 1, cols], ALU.add)
                else:
                    nc.vector.tensor_tensor(sums[:, 1, cols], b[:].indirect(l_n6[:, entries]), ga[:, 1, cols], ALU.add)
                nc.vector.tensor_tensor(res[:, cols], sums[:, 0, cols], sums[:, 1, cols], ALU.max)
                nc.sync.dma_start(out[r * P : (r + 1) * P, cols], res[:, cols])
